import numpy as np
CORES = [0,1,2,3,4,5,6,7]
N = 8
GROUPS = [[0,1,4,5],[2,3,6,7]]
def setup_inputs(rng):
    return {"x": rng.standard_normal((N, 128, 4), dtype=np.float32)}
def reference(x):
    y = np.empty((N, 128, 1), x.dtype)
    for g in GROUPS:
        s = x[g].max(axis=0)
        n = len(g); b = x.shape[2] // n
        for i, r in enumerate(g):
            y[r] = s[:, i * b:(i + 1) * b]
    return {"y": y}

@@ -1,0 +1,57 @@
+from concourse.bass import DstId, RemoteDMATransfer
+
+MAX = 2
+
+SCRATCH = {
+    "xs": ("sbuf", [128, 4], "float32"),
+    "land": ("sbuf", [128, 3], "float32"),
+    "res": ("sbuf", [128, 1], "float32"),
+}
+SEMAPHORES = ["loaded", "sent", "arrived", "result", "stored"]
+
+
+def rank_program(g, core, T, topo):
+    rank = T.rank_of(core)
+    if rank is None:
+        return
+    group = [gr for gr in T.tables["GROUPS"] if rank in gr][0]
+    n = len(group)
+    me = group.index(rank)
+    b = T.x.shape[1] // n
+    sem = T.sem
+
+    def core_of(m):
+        return T.cores[group[m]]
+
+    def dst_id(m):
+        rid, pid, _se = topo.addr(core_of(m))
+        return DstId(rid=rid, pnc=pid)
+
+    def cols(buf, k):
+        return buf[:, k * b:(k + 1) * b]
+
+    g.sync.dma_start(T.xs[:], T.x[:]).then_inc(sem.loaded, 16)
+    g.wait_ge(sem.loaded, 16)
+
+    mine = me ^ 1
+    copies = []
+    for j in range(n):
+        if j == mine:
+            continue
+        f = j ^ 1
+        copies.append(RemoteDMATransfer(
+            dst_ids=[dst_id(f)], dma_engine_mask=0xF << (4 * len(copies)), remote_sem=sem.arrived,
+            src=cols(T.xs, j), dst=cols(T.land, (me - f - 1) % n)))
+    g.remote_dma_fused(copies, local_sem=sem.sent)
+
+    g.wait_ge(sem.arrived, 4 * (n - 1))
+    g.remote_dma_fused([RemoteDMATransfer(
+        dst_ids=[dst_id(mine)], dma_engine_mask=topo.mask(core, core_of(mine)), remote_sem=sem.result,
+        srcs=[cols(T.xs, mine)] + [cols(T.land, k) for k in range(n - 1)], dsts=[T.res[:]], alu_op=MAX)],
+        local_sem=sem.sent)
+
+    g.sync.wait_ge(sem.result, 16)
+    g.sync.dma_start(T.y[:], T.res[:]).then_inc(sem.stored, 16)
+
+    g.wait_ge(sem.sent, 4 * (n - 1) + 16)
+    g.wait_ge(sem.stored, 16)

@@ -3,11 +3,11 @@ from concourse.bass import DstId, RemoteDMATransfer
 MAX = 2
 
 SCRATCH = {
-    "xs": ("sbuf", [128, 4], "float32"),
-    "land": ("sbuf", [128, 3], "float32"),
-    "res": ("sbuf", [128, 1], "float32"),
+    "xd": ("dram", [4, 128, 1], "float32"),
+    "land": ("dram", [3, 128, 1], "float32"),
+    "res": ("dram", [128, 1], "float32"),
 }
-SEMAPHORES = ["loaded", "sent", "arrived", "result", "stored"]
+SEMAPHORES = ["split_out", "split_own", "sent", "arrived", "result", "stored"]
 
 
 def rank_program(g, core, T, topo):
@@ -17,41 +17,33 @@ def rank_program(g, core, T, topo):
     group = [gr for gr in T.tables["GROUPS"] if rank in gr][0]
     n = len(group)
     me = group.index(rank)
-    b = T.x.shape[1] // n
+    mine = me ^ 1
+    out = [j for j in range(n) if j != mine]
     sem = T.sem
 
-    def core_of(m):
-        return T.cores[group[m]]
-
     def dst_id(m):
-        rid, pid, _se = topo.addr(core_of(m))
+        rid, pid, _se = topo.addr(T.cores[group[m]])
         return DstId(rid=rid, pnc=pid)
 
-    def cols(buf, k):
-        return buf[:, k * b:(k + 1) * b]
+    for j in out:
+        g.dma_start(T.xd[j], T.x[:, j:j + 1], allow_slow_non_contiguous=True).then_inc(sem.split_out, 16)
+    g.dma_start(T.xd[mine], T.x[:, mine:mine + 1], allow_slow_non_contiguous=True).then_inc(sem.split_own, 16)
 
-    g.sync.dma_start(T.xs[:], T.x[:]).then_inc(sem.loaded, 16)
-    g.wait_ge(sem.loaded, 16)
-
-    mine = me ^ 1
-    copies = []
-    for j in range(n):
-        if j == mine:
-            continue
-        f = j ^ 1
-        copies.append(RemoteDMATransfer(
-            dst_ids=[dst_id(f)], dma_engine_mask=0xF << (4 * len(copies)), remote_sem=sem.arrived,
-            src=cols(T.xs, j), dst=cols(T.land, (me - f - 1) % n)))
-    g.remote_dma_fused(copies, local_sem=sem.sent)
-
-    g.wait_ge(sem.arrived, 4 * (n - 1))
+    g.wait_ge(sem.split_out, 16 * len(out))
     g.remote_dma_fused([RemoteDMATransfer(
-        dst_ids=[dst_id(mine)], dma_engine_mask=topo.mask(core, core_of(mine)), remote_sem=sem.result,
-        srcs=[cols(T.xs, mine)] + [cols(T.land, k) for k in range(n - 1)], dsts=[T.res[:]], alu_op=MAX)],
+        dst_ids=[dst_id(j ^ 1)], dma_engine_mask=1 << k, remote_sem=sem.arrived,
+        src=T.xd[j], dst=T.land[(me - (j ^ 1) - 1) % n]) for k, j in enumerate(out)],
         local_sem=sem.sent)
 
-    g.sync.wait_ge(sem.result, 16)
+    g.wait_ge(sem.split_own, 16)
+    g.wait_ge(sem.arrived, n - 1)
+    g.remote_dma_fused([RemoteDMATransfer(
+        dst_ids=[dst_id(mine)], dma_engine_mask=1, remote_sem=sem.result,
+        srcs=[T.xd[mine]] + [T.land[k] for k in range(n - 1)], dsts=[T.res[:]], alu_op=MAX)],
+        local_sem=sem.sent)
+
+    g.sync.wait_ge(sem.result, 1)
     g.sync.dma_start(T.y[:], T.res[:]).then_inc(sem.stored, 16)
 
-    g.wait_ge(sem.sent, 4 * (n - 1) + 16)
+    g.wait_ge(sem.sent, len(out) + 1)
     g.wait_ge(sem.stored, 16)

from concourse.bass import DstId, RemoteDMATransfer

MAX = 2

SCRATCH = {
    "xd": ("dram", [4, 128, 1], "float32"),
    "land": ("dram", [3, 128, 1], "float32"),
    "res": ("dram", [128, 1], "float32"),
}
SEMAPHORES = ["split_out", "split_own", "sent", "arrived", "result", "stored"]


def rank_program(g, core, T, topo):
    rank = T.rank_of(core)
    if rank is None:
        return
    group = [gr for gr in T.tables["GROUPS"] if rank in gr][0]
    n = len(group)
    me = group.index(rank)
    mine = me ^ 1
    out = [j for j in range(n) if j != mine]
    sem = T.sem

    def dst_id(m):
        rid, pid, _se = topo.addr(T.cores[group[m]])
        return DstId(rid=rid, pnc=pid)

    for j in out:
        g.dma_start(T.xd[j], T.x[:, j:j + 1], allow_slow_non_contiguous=True).then_inc(sem.split_out, 16)
    g.dma_start(T.xd[mine], T.x[:, mine:mine + 1], allow_slow_non_contiguous=True).then_inc(sem.split_own, 16)

    g.wait_ge(sem.split_out, 16 * len(out))
    g.remote_dma_fused([RemoteDMATransfer(
        dst_ids=[dst_id(j ^ 1)], dma_engine_mask=1 << k, remote_sem=sem.arrived,
        src=T.xd[j], dst=T.land[(me - (j ^ 1) - 1) % n]) for k, j in enumerate(out)],
        local_sem=sem.sent)

    g.wait_ge(sem.split_own, 16)
    g.wait_ge(sem.arrived, n - 1)
    g.remote_dma_fused([RemoteDMATransfer(
        dst_ids=[dst_id(mine)], dma_engine_mask=1, remote_sem=sem.result,
        srcs=[T.xd[mine]] + [T.land[k] for k in range(n - 1)], dsts=[T.res[:]], alu_op=MAX)],
        local_sem=sem.sent)

    g.sync.wait_ge(sem.result, 1)
    g.sync.dma_start(T.y[:], T.res[:]).then_inc(sem.stored, 16)

    g.wait_ge(sem.sent, len(out) + 1)
    g.wait_ge(sem.stored, 16)
